import numpy as np
import ml_dtypes


def mxq(x, axis, fmt="e4m3"):
    dtype, down = {"e4m3": (ml_dtypes.float8_e4m3fn, 7), "e5m2": (ml_dtypes.float8_e5m2, 14)}[fmt]
    v = np.moveaxis(np.asarray(x, np.float32).astype(ml_dtypes.bfloat16).astype(np.float64), axis, -1)
    blocks = v.reshape(v.shape[:-1] + (-1, 32))
    amax = np.abs(blocks).max(-1, keepdims=True)
    byte = np.maximum(np.where(amax > 0, np.frexp(amax)[1] - 1 + 127, 0) - down, 1)
    scale = np.exp2(byte - 127.0)
    codes = (blocks / scale).astype(np.float32).astype(dtype).astype(np.float64)
    return np.moveaxis((codes * scale).reshape(v.shape), -1, axis)


WIDE = False


def mx_kscale(k):
    if not WIDE:
        return np.ones(k)
    levels = np.array([10, -10, 5, -5, 0])
    if k % 512:
        return np.exp2(np.random.permutation(np.resize(levels, k // 32))).repeat(32)
    a = np.empty((k // 512, 16))
    for p in range(k // 512):
        a[p, :8] = np.random.permutation(np.resize(levels, 8))
        for g in range(8):
            far = levels[np.abs(levels - a[p, g]) >= 10]
            a[p, g + 8] = far[np.random.randint(len(far))]
    return np.exp2(a.ravel()).repeat(32)


def f64(x):
    return np.asarray(x).astype(np.float64)


def striped(idx):
    return np.tile(idx.reshape(-1, 16).T, (8, 1)).astype(np.uint16)


def unstriped(offs):
    return offs[:16].T.reshape(-1).astype(np.int64)


E2M1 = np.array([0.0, 0.5, 1.0, 1.5, 2.0, 3.0, 4.0, 6.0, -0.0, -0.5, -1.0, -1.5, -2.0, -3.0, -4.0, -6.0])


def pack_weight(w, fmt):
    k, n = w.shape
    w = f64(np.asarray(w, np.float32).astype(ml_dtypes.bfloat16)).reshape(k // 32, 32, n)
    amax = np.abs(w).max(1)
    if fmt == "e4m3":
        byte = np.frexp(amax)[1] - 1 + 127 - 7
    else:
        mant, ex = np.frexp(amax / 6.0)
        byte = np.where(mant > 0.5, ex, ex - 1) + 127
    byte = np.clip(np.where(amax > 0, byte, 1), 1, 254)
    scaled = (w * np.exp2(127.0 - byte)[:, None, :]).reshape(k, n).astype(np.float32)
    by_word = np.ascontiguousarray(scaled.reshape(k // 512, 128, 4, n).transpose(0, 1, 3, 2))
    if fmt == "e4m3":
        words = by_word.astype(ml_dtypes.float8_e4m3fn).view(np.uint8)
    else:
        c = by_word.astype(ml_dtypes.float4_e2m1fn).view(np.uint8) & 0xF
        words = (c[..., 0::2] | (c[..., 1::2] << 4)).reshape(k // 512, 128, 2 * n)
    return np.ascontiguousarray(words), np.ascontiguousarray(byte.astype(np.uint8).reshape(k // 512, 16, n))


def unpack_weight(words, scales, fmt):
    g, _, n = scales.shape
    words = np.ascontiguousarray(words).reshape(g, 128, n, -1)
    if fmt == "e4m3":
        vals = words.view(ml_dtypes.float8_e4m3fn).astype(np.float64)
    else:
        nib = np.empty((g, 128, n, 4), np.uint8)
        nib[..., 0::2] = words & 0xF
        nib[..., 1::2] = words >> 4
        vals = E2M1[nib]
    vals = vals * np.repeat(np.exp2(scales.astype(np.float64) - 127.0), 8, axis=1)[..., None]
    return vals.transpose(0, 1, 3, 2).reshape(g * 512, n)


def gelu(v):
    return 0.5 * v * (1.0 + np.tanh(np.sqrt(2.0 / np.pi) * (v + 0.044715 * v**3)))


K, M, H, N, T, T3, S, T2, P = 1536, 512, 1024, 512, 2048, 1024, 512, 2048, 512

def setup_inputs():
    n = np.random.standard_normal
    s, s2, u = mx_kscale(K)[:, None], mx_kscale(M)[:, None], mx_kscale(H)[:, None]
    perm = np.random.permutation(T2)
    d = {}
    d["tab_words"], d["tab_scales"] = pack_weight(n((K, T)) * s, "e4m3")
    d["tab2_words"], d["tab2_scales"] = pack_weight(n((M, T3)) * s2, "e4m3")
    d["offs"] = striped(np.random.permutation(T)[:S])
    d["offs2"] = striped(np.random.permutation(T3)[:S])
    d["offs3"] = striped(perm[:S])
    d["offs4"] = striped(perm[S:2 * S])
    d["offs5"] = striped(np.random.permutation(T2)[:P])
    d["w1"] = (n((K, H)) * (1.5 / K ** 0.5) / s).astype(np.float32)
    d["master"] = (1.2 * n((H, S))).astype(np.float32)
    d["w2"] = (n((M, H)) * (1.1 / M ** 0.5) / s2).astype(np.float32)
    d["w3_words"], d["w3_scales"] = pack_weight(n((M, H)) * (1.2 / M ** 0.5) / s2, "e4m3")
    d["wg1"] = np.exp(0.3 * n((128, S))).astype(np.float32)
    d["wg2"] = np.exp(0.3 * n((128, S))).astype(np.float32)
    d["page0"] = (1.3 * n((H, T2))).astype(np.float32)
    d["gain"] = (np.exp(0.3 * n(H)) * u[:, 0]).astype(np.float32)
    d["w4_words"], d["w4_scales"] = pack_weight(n((H, N)) * (2.0 / H ** 0.5) / u, "e2m1")
    d["w5"] = (n((K, N)) * (0.7 / K ** 0.5) / s).astype(np.float32)
    d["lots"] = (0.7 * n((N, P))).astype(np.float32)
    return d

def reference(tab_words, tab_scales, tab2_words, tab2_scales, offs, offs2, offs3, offs4, offs5, w1, master, w2, w3_words, w3_scales, wg1, wg2, page0, gain, w4_words, w4_scales, w5, lots):
    v = unpack_weight(tab_words, tab_scales, "e4m3")[:, unstriped(offs)]
    v2 = unpack_weight(tab2_words, tab2_scales, "e4m3")[:, unstriped(offs2)]
    z = (mxq(f64(w1), 0, "e4m3").T @ v) + f64(master)
    h1 = z / (1.0 + np.exp(-z))
    swing = np.abs(mxq(f64(w2), 0, "e4m3").T @ v2)
    h2 = swing * (unpack_weight(w3_words, w3_scales, "e4m3").T @ v2)
    page = f64(page0).copy()
    page[:, unstriped(offs3)] = np.tile(f64(wg1), (H // 128, 1)) * h1
    page[:, unstriped(offs4)] = np.tile(f64(wg2), (H // 128, 1)) * h2
    x = np.tanh(page[:, unstriped(offs5)]) * f64(gain)[:, None]
    xq = mxq(x, 0, "e4m3")
    w4 = unpack_weight(w4_words, w4_scales, "e2m1")
    w5q = mxq(f64(w5), 0, "e4m3")
    out = (w4.T @ xq + w5q.T @ v) + f64(lots)
    return out

@@ -1,0 +1,434 @@
+from contextlib import ExitStack
+
+import concourse.mybir as mybir
+from concourse.masks import make_identity
+
+K, M, H, N, T, T3, S, T2 = 1536, 512, 1024, 512, 2048, 1024, 512, 2048
+FLOPS = 2 * S * (K * H + 2 * M * H + H * N + K * N)
+
+F32 = mybir.dt.float32
+BF16 = mybir.dt.bfloat16
+I32 = mybir.dt.int32
+U32 = mybir.dt.uint32
+U16 = mybir.dt.uint16
+U8 = mybir.dt.uint8
+FP8X4 = mybir.dt.float8_e4m3fn_x4
+FP4X4 = mybir.dt.float4_e2m1fn_x4
+ACT = mybir.ActivationFunctionType
+MULT = mybir.AluOpType.mult
+ADD = mybir.AluOpType.add
+
+P = 128
+PACK = 4
+PASS = P * PACK
+K_PASSES = K // PASS
+R_PASSES = H // PASS
+QUADS = 4
+QUAD = 32
+HALF = S // 2
+HEAD_VECTOR_ROWS = 56
+FIRST_PASS = 1
+VECTOR_COLS = 160
+
+
+def tile_list_groove_fault_ledger_kernel(
+    tc, tab_words, tab_scales, tab2_words, tab2_scales, offs, offs2, offs3, offs4, offs5,
+    w1, master, w2, w3_words, w3_scales, wg1, wg2, page0, gain, w4_words, w4_scales, w5, lots, out,
+):
+    nc = tc.nc
+    with ExitStack() as ctx:
+        lists = ctx.enter_context(tc.tile_pool(name="lists", bufs=1))
+        keep = ctx.enter_context(tc.tile_pool(name="keep", bufs=1))
+        ring = ctx.enter_context(tc.tile_pool(name="ring", bufs=1))
+        psum = ctx.enter_context(tc.psum_pool(name="psum", bufs=1))
+
+        banks = [psum.tile([P, S], F32, name="bank%d" % b) for b in range(8)]
+
+        def held(shape, dtype, name):
+            return keep.tile(shape, dtype, name=name, align_bytes=64)
+
+        turns = {}
+
+        def rotating(kind, depth, shape, dtype, slot=None):
+            if slot is None:
+                slot = turns.get(kind, 0) % depth
+                turns[kind] = slot + 1
+            name = "%s%d" % (kind, slot)
+            return ring.tile(shape, dtype, name=name, tag=name, align_bytes=64)
+
+        def big(shape, dtype):
+            return rotating("big", 8, shape, dtype)
+
+        def small(shape, dtype):
+            return rotating("small", 4, shape, dtype)
+
+        def staged(shape, dtype):
+            return rotating("staged", 3, shape, dtype)
+
+        def words_tile(dtype):
+            return rotating("codes", 8, [P, S], dtype)
+
+        tab2_s = held([P, T3], U8, "tab2_s")
+        w3_s = held([P, H], U8, "w3_s")
+        tab_s = held([P, T], U8, "tab_s")
+        nc.gpsimd.memset(tab2_s[:].bitcast(I32), 0)
+        nc.gpsimd.memset(w3_s[:].bitcast(I32), 0)
+
+        def load_list(src, name):
+            t = lists.tile([P, S // 16], U16, name=name)
+            nc.sync.dma_start(t[:], src)
+            return t
+
+        def load_scale_rows(queue, dst, src):
+            for q in range(QUADS):
+                queue.dma_start(dst[QUAD * q : QUAD * q + 4, :].bitcast(I32), src[4 * q : 4 * q + 4, :].bitcast(I32))
+
+        def load_weight(w, kp, c0):
+            raw = big([P, PACK, S], F32)
+            nc.sync.dma_start(raw[:], w[PASS * kp : PASS * (kp + 1), c0 : c0 + S].rearrange("(p j) c -> p j c", j=PACK))
+            return raw
+
+        page_rows = page0.rearrange("(a p t) s -> a t p s", a=R_PASSES, t=PACK)
+        master_rows = master.rearrange("(a p t) s -> a t p s", a=R_PASSES, t=PACK)
+
+        def load_page(i):
+            t = keep.tile([P, T2], F32, name="page%d" % i)
+            nc.sync.dma_start(t[:], page_rows[i // PACK][i % PACK])
+            return t
+
+        def load_master(i):
+            t = small([P, S], F32)
+            nc.sync.dma_start(t[:], master_rows[i // PACK][i % PACK])
+            return t
+
+        def load_wg(src, t0, t1, t):
+            rows = src.rearrange("(q t) j -> q t j", t=PACK)
+            for q in (0, 2, 1, 3):
+                nc.sync.dma_start(t[QUAD * q : QUAD * (q + 1), :, :], rows[:, t0:t1, :])
+            return t
+
+        def load_tab(kp):
+            t = big([P, T], U32)
+            nc.sync.dma_start(t[:].bitcast(I32), tab_words[kp].rearrange("p n t -> p (n t)").bitcast(I32))
+            return t
+
+        pages, masters, tabs = {}, {}, {}
+        w1_raw, w2_raw, w5_raw = {}, {}, {}
+
+        nc.gpsimd.memset(tab_s[:].bitcast(I32), 0)
+        w4_s = held([P, R_PASSES, N], U8, "w4_s")
+        nc.gpsimd.memset(w4_s[:].bitcast(I32), 0)
+        ident = held([P, P], F32, "ident")
+        make_identity(nc, ident[:])
+
+        idx2 = load_list(offs2, "idx2")
+        tab2_w = staged([P, T3], U32)
+        nc.sync.dma_start(tab2_w[:].bitcast(I32), tab2_words[0].rearrange("p n t -> p (n t)").bitcast(I32))
+        load_scale_rows(nc.sync, tab2_s, tab2_scales[0])
+        w2_raw[0] = load_weight(w2, 0, 0)
+        w3_raw = rotating("staged", 3, [P, H], I32, 2)
+        nc.sync.dma_start(w3_raw[:], w3_words[0].rearrange("p n t -> p (n t)").bitcast(I32))
+        load_scale_rows(nc.sync, w3_s, w3_scales[0])
+        pages[0] = load_page(0)
+        wg2_first = load_wg(wg2, 0, 1, held([P, 1, S], F32, "wg2_first"))
+        idx4 = load_list(offs4, "idx4")
+        wg2_rest = load_wg(wg2, 1, PACK, rotating("gate", 1, [P, PACK - 1, S], F32))
+        pages[1] = load_page(1)
+        w2_raw[1] = load_weight(w2, 0, S)
+        pages[2] = load_page(2)
+        idx = load_list(offs, "idx")
+        tabs[0] = load_tab(0)
+        pages[3] = load_page(3)
+        idx3 = load_list(offs3, "idx3")
+        tabs[1] = load_tab(1)
+        idx5 = load_list(offs5, "idx5")
+        pages[4] = load_page(4)
+        w1_raw[0, 0] = load_weight(w1, 0, 0)
+        for q in range(QUADS):
+            nc.sync.dma_start(
+                tab_s[QUAD * q : QUAD * q + 4 * K_PASSES, :].bitcast(I32), tab_scales[:, 4 * q : 4 * q + 4, :].bitcast(I32)
+            )
+        tabs[2] = load_tab(2)
+        pages[5] = load_page(5)
+        gain_t = held([P, R_PASSES, PACK], F32, "gain_t")
+        nc.sync.dma_start(gain_t[:], gain.rearrange("(a p t) -> p a t", a=R_PASSES, t=PACK))
+        w1_raw[0, 1] = load_weight(w1, 1, 0)
+        w1_raw[0, 2] = load_weight(w1, 2, 0)
+        masters[0] = load_master(0)
+        masters[1] = load_master(1)
+        pages[6] = load_page(6)
+        for q in range(QUADS):
+            nc.sync.dma_start(
+                w4_s[QUAD * q : QUAD * q + 4, :, :].bitcast(I32),
+                w4_scales[:, 4 * q : 4 * q + 4, :].rearrange("a r n -> r a n").bitcast(I32),
+            )
+        masters[2] = load_master(2)
+        masters[3] = load_master(3)
+        pages[7] = load_page(7)
+        wg1_lo = load_wg(wg1, 0, 2, held([P, 2, S], F32, "wg1_lo"))
+        for kp in range(K_PASSES):
+            w1_raw[1, kp] = load_weight(w1, kp, S)
+        w5_raw[0] = load_weight(w5, 0, 0)
+        master_hi = big([P, PACK, S], F32)
+        nc.sync.dma_start(master_hi[:], master[PASS:H, :].rearrange("(p t) j -> p t j", t=PACK))
+        for i in range(PACK):
+            masters[PACK + i] = master_hi[:, i, :]
+        wg1_hi = load_wg(wg1, 2, 4, big([P, 2, S], F32))
+        w5_raw[1] = load_weight(w5, 1, 0)
+        w5_raw[2] = load_weight(w5, 2, 0)
+        lots_t = rotating("gate", 1, [P, N // P, S], F32)
+        nc.sync.dma_start(lots_t[:], lots.rearrange("(b p) j -> p b j", p=P))
+        w4_w = small([P, R_PASSES, 2 * N], U8)
+        nc.sync.dma_start(w4_w[:].bitcast(I32), w4_words.rearrange("a p b -> p a b").bitcast(I32))
+
+        def quantize(grouped):
+            codes = words_tile(U32)
+            scales = rotating("scales", 6, [P, S], U8)
+            nc.vector.quantize_mx(out=codes[:].bitcast(FP8X4), scales=scales[:], in_=grouped[:])
+            return codes, scales
+
+        def interleave(copy, grouped, planes, c0, c1, base=0):
+            dst = grouped[:, PACK * (c0 - base) : PACK * (c1 - base)].rearrange("p (c i j) -> p c j i", i=4, j=PACK)
+            copy(dst, planes[:, :, c0:c1].rearrange("p j (c i) -> p c j i", i=4))
+
+        def deal(copy, grouped, raw, m0, m1):
+            dst = grouped[:].rearrange("p (t m j) -> p m j t", t=PACK, j=PACK)
+            copy(dst[:, m0:m1, :, :], raw[:].rearrange("p j (m t) -> p m j t", t=PACK)[:, m0:m1, :, :])
+
+        def bf16_room(spent, upper=0):
+            return spent[:].rearrange("p j c -> p (j c)").bitcast(BF16)[:, PACK * S * upper : PACK * S * (upper + 1)]
+
+        def quantize_plain(raw, grouped):
+            interleave(nc.scalar.copy, grouped, raw[:], 0, S)
+            return quantize(grouped)
+
+        def gather(window, offsets, dtype, name):
+            t = held([P, S], dtype, name)
+            nc.vector.tensor_copy(t[:], window[:].indirect(offsets[:]))
+            return t
+
+        def mx(bank, lhs, lhs_s, rhs, rhs_s, start, stop, lhs_dtype=FP8X4):
+            nc.tensor.matmul_mx(
+                out=bank, lhsT=lhs.bitcast(lhs_dtype), lhsT_scale=lhs_s, rhs=rhs.bitcast(FP8X4), rhs_scale=rhs_s,
+                start=start, stop=stop,
+            )
+
+        v2_w = gather(tab2_w, idx2, U32, "v2_w")
+        v2_s = gather(tab2_s, idx2, U8, "v2_s")
+
+        w3_dealt = held([P, R_PASSES, S], I32, "w3_dealt")
+
+        def prepare_heat(a):
+            grouped = staged([P, PACK * S], BF16)
+            if a == 0:
+                deal(nc.vector.tensor_copy, grouped, w2_raw[a], 0, HEAD_VECTOR_ROWS)
+                deal(nc.scalar.copy, grouped, w2_raw[a], HEAD_VECTOR_ROWS, P)
+            else:
+                deal(nc.scalar.copy, grouped, w2_raw[a], 0, P)
+            w2_q = quantize(grouped)
+            words = w3_dealt[:, a, :]
+            nc.vector.tensor_copy(
+                words.rearrange("p (t m) -> p t m", t=PACK), w3_raw[:, S * a : S * (a + 1)].rearrange("p (m t) -> p t m", t=PACK)
+            )
+            planes = held([P, S], U8, "w3_s_dealt%d" % a)
+            nc.vector.tensor_copy(
+                planes[:].rearrange("p (t m) -> p t m", t=PACK),
+                w3_s[:, S * a : S * (a + 1)].rearrange("p (m t) -> p t m", t=PACK),
+            )
+            return w2_q, (words, planes)
+
+        def heat_tile(i, w2_q, w3_q, product=None):
+            cols = slice(P * (i % PACK), P * (i % PACK + 1))
+            wg = wg2_first[:, 0, :] if i % PACK == 0 else wg2_rest[:, i % PACK - 1, :]
+            first = 2 * i if i < PACK else 2 * (i % 2)
+            bank_a, bank_b = banks[first], banks[first + 1]
+            mx(bank_a[:], w2_q[0][:, cols], w2_q[1][:, cols], v2_w[:], v2_s[:], True, True)
+            mx(bank_b[:], w3_q[0][:, cols], w3_q[1][:, cols], v2_w[:], v2_s[:], True, True)
+            h2 = rotating("h2", 4, [P, S], F32)
+            nc.scalar.activation(h2[:], bank_a[:], ACT.Abs)
+            if product is None:
+                product = h2[:]
+            nc.vector.tensor_tensor(product, bank_b[:], h2[:], MULT)
+            nc.vector.tensor_tensor(pages[i][:].indirect(idx4[:]), product, wg, MULT)
+
+        v_w = {}
+        heat_w = prepare_heat(0)
+        heat_tile(0, *heat_w)
+        heat_tile(1, *heat_w)
+        heat_w_next = prepare_heat(1)
+        heat_tile(2, *heat_w)
+        v_w[0] = gather(tabs[0], idx, U32, "v_w0")
+        heat_tile(3, *heat_w)
+        v_w[1] = gather(tabs[1], idx, U32, "v_w1")
+        heat_tile(4, *heat_w_next)
+        v_s = gather(tab_s, idx, U8, "v_s")
+        w1_q = {}
+        w1_q[0, 0] = quantize_plain(w1_raw[0, 0], staged([P, PACK * S], BF16))
+        v_w[2] = gather(tabs[2], idx, U32, "v_w2")
+        heat_tile(5, *heat_w_next)
+        w1_q[0, 1] = quantize_plain(w1_raw[0, 1], staged([P, PACK * S], BF16))
+        grouped = staged([P, PACK * S], BF16)
+        w1_q[0, 2] = quantize_plain(w1_raw[0, 2], grouped)
+        late = grouped[:].bitcast(F32)
+        heat_tile(6, *heat_w_next, late[:, 0:S])
+        heat_tile(7, *heat_w_next, late[:, S : 2 * S])
+
+        work = held([P, PACK * S], F32, "work")
+        y_t = work[:].rearrange("p (b t q) -> p b t q", b=S // P, t=PACK)
+        x_planes = work[:].rearrange("p (t j) -> p t j", t=PACK)
+
+        def turn_master(i, turned):
+            bank = banks[i % PACK]
+            for b in range(S // P):
+                nc.tensor.transpose(bank[:, P * b : P * (b + 1)], masters[i][:, P * b : P * (b + 1)], ident[:])
+            nc.scalar.copy(turned, bank[:])
+
+        def stamper_products(a):
+            for kp in range(K_PASSES):
+                codes, scales = w1_q[a, kp]
+                for b in range(S // P):
+                    cols = slice(P * b, P * (b + 1))
+                    mx(banks[4 + b][:], v_w[kp][:, cols], v_s[4 * kp : P, cols], codes[:], scales[:], kp == 0, kp == K_PASSES - 1)
+            for b in range(S // P):
+                nc.scalar.copy(y_t[:, b, :, :], banks[4 + b][:].rearrange("p (q t) -> p t q", t=PACK))
+
+        def stamper_sum(i, turned):
+            t = i % PACK
+            bank = banks[t]
+            for b in range(S // P):
+                cols = slice(P * b, P * (b + 1))
+                nc.tensor.matmul(bank[:, cols], turned[:, cols], ident[:], is_transpose=True, start=True, stop=False)
+                nc.tensor.matmul(bank[:, cols], y_t[:, b, t, :], ident[:], is_transpose=True, start=False, stop=True)
+
+        def stamper_tile(i, turned, h1=None):
+            stamper_sum(i, turned)
+            if h1 is None:
+                h1 = rotating("h1", 4, [P, S], F32)[:]
+            nc.scalar.activation(h1, banks[i % PACK][:], ACT.Silu)
+            return h1
+
+        def put(i, h1):
+            t = i % PACK
+            wg = wg1_lo if t < 2 else wg1_hi
+            nc.vector.tensor_tensor(pages[i][:].indirect(idx3[:]), h1, wg[:, t % 2, :], MULT)
+
+        def fetch(i, picked=None):
+            if picked is None:
+                picked = rotating("picked", 4, [P, S], F32)[:]
+            nc.vector.tensor_copy(picked, pages[i][:].indirect(idx5[:]))
+            return picked
+
+        def listen(i, picked, c0, c1):
+            a, t = i // PACK, i % PACK
+            nc.scalar.activation(x_planes[:, t, c0:c1], picked[:, c0:c1], ACT.Tanh)
+            nc.scalar.activation(x_planes[:, t, c0:c1], x_planes[:, t, c0:c1], ACT.Copy, scale=gain_t[:, a, t : t + 1])
+
+        h1s, picks = {}, {}
+        turned_lo = w1_raw[0, 2]
+        turned = [turned_lo[:, t, :] for t in range(PACK)]
+        turn_master(0, turned[0])
+        stamper_products(0)
+        for i in (1, 2, 3):
+            turn_master(i, turned[i])
+        for i in (0, 1):
+            put(i, stamper_tile(i, turned[i]))
+        w1_q[1, 0] = quantize_plain(w1_raw[1, 0], bf16_room(w1_raw[0, 2]))
+        w1_q[1, 1] = quantize_plain(w1_raw[1, 1], bf16_room(w1_raw[1, 0]))
+        w1_q[1, 2] = quantize_plain(w1_raw[1, 2], bf16_room(w1_raw[1, 1]))
+        late = w1_raw[1, 2]
+        for i in (0, 1):
+            picks[i] = fetch(i, late[:, i, :])
+        for i in (2, 3):
+            put(i, stamper_tile(i, turned[i], late[:, i, :]))
+        for i in (2, 3):
+            picks[i] = fetch(i)
+        turned_hi = w1_raw[1, 1]
+        turned = [turned_hi[:, t, :] for t in range(PACK)]
+        turn_master(4, turned[0])
+        stamper_products(1)
+        for i in range(4, 7):
+            if i > 4:
+                turn_master(i, turned[i - 4])
+            h1s[i] = stamper_tile(i, turned[i - 4], late[:, i - 2, :] if i < 6 else None)
+        turn_master(7, turned[3])
+        stamper_sum(7, turned[3])
+
+        def sum_range(b, half):
+            c0 = HALF * (b % 2)
+            return banks[2 * half + b // 2], c0
+
+        def ledger_passes(kp, w5_q):
+            for half in range(2):
+                cols = slice(HALF * half, HALF * (half + 1))
+                for b in range(N // P):
+                    bank, c0 = sum_range(b, half)
+                    rows = slice(P * b, P * (b + 1))
+                    mx(
+                        bank[:, c0 : c0 + HALF], w5_q[0][:, rows], w5_q[1][:, rows],
+                        v_w[kp][:, cols], v_s[4 * kp : P, cols], kp == FIRST_PASS and b % 2 == 0, False,
+                    )
+
+        def listener_passes(a, x_q, half):
+            for b in range(N // P):
+                bank, c0 = sum_range(b, half)
+                for piece in range(HALF // P):
+                    cols = slice(HALF * half + P * piece, HALF * half + P * (piece + 1))
+                    mx(
+                        bank[:, c0 + P * piece : c0 + P * (piece + 1)],
+                        w4_w[:, a, 2 * P * b : 2 * P * (b + 1)], w4_s[:, a, P * b : P * (b + 1)],
+                        x_q[0][:, cols], x_q[1][:, cols],
+                        False, a == R_PASSES - 1 and b % 2 == 1 and piece == HALF // P - 1, FP4X4,
+                    )
+
+        w5_q = [
+            quantize_plain(w5_raw[0], bf16_room(master_hi, 1)),
+            quantize_plain(w5_raw[1], bf16_room(turned_hi, 1)),
+            quantize_plain(w5_raw[2], bf16_room(w5_raw[1])),
+        ]
+        for i in range(4):
+            listen(i, picks[i], 0, S)
+        grouped = staged([P, PACK * S], BF16)
+        interleave(nc.scalar.copy, grouped, x_planes, 0, S)
+        last = x_planes[:, PACK - 1, :]
+        nc.scalar.activation(last, banks[PACK - 1][:], ACT.Silu)
+        for i in range(4, 7):
+            put(i, h1s[i])
+        x_q = quantize(grouped)
+        for kp in (1, 2, 0):
+            ledger_passes(kp, w5_q[kp])
+        for half in range(2):
+            listener_passes(0, x_q, half)
+        for i in (4, 5):
+            listen(i, fetch(i), 0, S)
+        picked = rotating("picked", 4, [P, S], F32)
+        fetch(6, x_planes[:, 2, :])
+        nc.scalar.activation(picked[:], x_planes[:, 2, :], ACT.Tanh)
+        nc.scalar.activation(x_planes[:, 2, :], picked[:], ACT.Copy, scale=gain_t[:, 1, 2:3])
+        put(7, last)
+        squashed = rotating("picked", 4, [P, HALF], F32)
+        for half in range(2):
+            c0 = HALF * half
+            nc.vector.tensor_copy(picked[:, c0 : c0 + HALF], pages[7][:].indirect(idx5[:, c0 // 16 : (c0 + HALF) // 16]))
+            nc.scalar.activation(squashed[:], picked[:, c0 : c0 + HALF], ACT.Tanh)
+            nc.scalar.activation(x_planes[:, 3, c0 : c0 + HALF], squashed[:], ACT.Copy, scale=gain_t[:, 1, 3:4])
+        grouped = staged([P, PACK * S], BF16)
+        x_q = words_tile(U32), rotating("scales", 6, [P, S], U8)
+        for half in range(2):
+            c0 = HALF * half
+            split = c0 + (HALF if half == 0 else VECTOR_COLS)
+            interleave(nc.vector.tensor_copy, grouped, x_planes, c0, split, c0)
+            if split < c0 + HALF:
+                interleave(nc.scalar.copy, grouped, x_planes, split, c0 + HALF, c0)
+            nc.vector.quantize_mx(
+                out=x_q[0][:, c0 : c0 + HALF].bitcast(FP8X4), scales=x_q[1][:, c0 : c0 + HALF],
+                in_=grouped[:, 0 : PACK * HALF],
+            )
+            listener_passes(1, x_q, half)
+        out_rows = out.rearrange("(b p) j -> p b j", p=P)
+        for half in range(2):
+            cols = slice(HALF * half, HALF * (half + 1))
+            for pair in range(2):
+                rows = slice(2 * pair, 2 * pair + 2)
+                sums = banks[2 * half + pair][:].rearrange("p (b j) -> p b j", b=2)
+                nc.vector.tensor_tensor(lots_t[:, rows, cols], sums, lots_t[:, rows, cols], ADD)
+                nc.sync.dma_start(out_rows[:, rows, cols], lots_t[:, rows, cols])

@@ -27,7 +27,6 @@ QUADS = 4
 QUAD = 32
 HALF = S // 2
 HEAD_VECTOR_ROWS = 56
-FIRST_PASS = 1
 VECTOR_COLS = 160
 
 
@@ -132,54 +131,37 @@ def tile_list_groove_fault_ledger_kernel(
         pages[0] = load_page(0)
         wg2_first = load_wg(wg2, 0, 1, held([P, 1, S], F32, "wg2_first"))
         idx4 = load_list(offs4, "idx4")
-        wg2_rest = load_wg(wg2, 1, PACK, rotating("gate", 1, [P, PACK - 1, S], F32))
+        wg2_rows = small([P, S], F32)
+        nc.sync.dma_start(wg2_rows[:], wg2)
         pages[1] = load_page(1)
-        w2_raw[1] = load_weight(w2, 0, S)
         pages[2] = load_page(2)
+        w2_raw[1] = load_weight(w2, 0, S)
         idx = load_list(offs, "idx")
         tabs[0] = load_tab(0)
         pages[3] = load_page(3)
+        wg1_rows = small([P, S], F32)
+        nc.sync.dma_start(wg1_rows[:], wg1)
         idx3 = load_list(offs3, "idx3")
         tabs[1] = load_tab(1)
         idx5 = load_list(offs5, "idx5")
         pages[4] = load_page(4)
-        w1_raw[0, 0] = load_weight(w1, 0, 0)
         for q in range(QUADS):
             nc.sync.dma_start(
                 tab_s[QUAD * q : QUAD * q + 4 * K_PASSES, :].bitcast(I32), tab_scales[:, 4 * q : 4 * q + 4, :].bitcast(I32)
             )
         tabs[2] = load_tab(2)
+        w1_raw[0, 0] = load_weight(w1, 0, 0)
         pages[5] = load_page(5)
         gain_t = held([P, R_PASSES, PACK], F32, "gain_t")
         nc.sync.dma_start(gain_t[:], gain.rearrange("(a p t) -> p a t", a=R_PASSES, t=PACK))
         w1_raw[0, 1] = load_weight(w1, 1, 0)
-        w1_raw[0, 2] = load_weight(w1, 2, 0)
-        masters[0] = load_master(0)
-        masters[1] = load_master(1)
         pages[6] = load_page(6)
-        for q in range(QUADS):
-            nc.sync.dma_start(
-                w4_s[QUAD * q : QUAD * q + 4, :, :].bitcast(I32),
-                w4_scales[:, 4 * q : 4 * q + 4, :].rearrange("a r n -> r a n").bitcast(I32),
-            )
+        masters[0] = load_master(0)
+        w1_raw[0, 2] = load_weight(w1, 2, 0)
+        pages[7] = load_page(7)
+        masters[1] = load_master(1)
         masters[2] = load_master(2)
         masters[3] = load_master(3)
-        pages[7] = load_page(7)
-        wg1_lo = load_wg(wg1, 0, 2, held([P, 2, S], F32, "wg1_lo"))
-        for kp in range(K_PASSES):
-            w1_raw[1, kp] = load_weight(w1, kp, S)
-        w5_raw[0] = load_weight(w5, 0, 0)
-        master_hi = big([P, PACK, S], F32)
-        nc.sync.dma_start(master_hi[:], master[PASS:H, :].rearrange("(p t) j -> p t j", t=PACK))
-        for i in range(PACK):
-            masters[PACK + i] = master_hi[:, i, :]
-        wg1_hi = load_wg(wg1, 2, 4, big([P, 2, S], F32))
-        w5_raw[1] = load_weight(w5, 1, 0)
-        w5_raw[2] = load_weight(w5, 2, 0)
-        lots_t = rotating("gate", 1, [P, N // P, S], F32)
-        nc.sync.dma_start(lots_t[:], lots.rearrange("(b p) j -> p b j", p=P))
-        w4_w = small([P, R_PASSES, 2 * N], U8)
-        nc.sync.dma_start(w4_w[:].bitcast(I32), w4_words.rearrange("a p b -> p a b").bitcast(I32))
 
         def quantize(grouped):
             codes = words_tile(U32)
@@ -192,14 +174,18 @@ def tile_list_groove_fault_ledger_kernel(
             copy(dst, planes[:, :, c0:c1].rearrange("p j (c i) -> p c j i", i=4))
 
         def deal(copy, grouped, raw, m0, m1):
-            dst = grouped[:].rearrange("p (t m j) -> p m j t", t=PACK, j=PACK)
-            copy(dst[:, m0:m1, :, :], raw[:].rearrange("p j (m t) -> p m j t", t=PACK)[:, m0:m1, :, :])
+            dst = grouped[:].rearrange("p (t m j) -> p m t j", t=PACK, j=PACK)
+            copy(dst[:, m0:m1, :, :], raw[:].rearrange("p j (m t) -> p m t j", t=PACK)[:, m0:m1, :, :])
 
         def bf16_room(spent, upper=0):
             return spent[:].rearrange("p j c -> p (j c)").bitcast(BF16)[:, PACK * S * upper : PACK * S * (upper + 1)]
 
         def quantize_plain(raw, grouped):
             interleave(nc.scalar.copy, grouped, raw[:], 0, S)
+            return quantize(grouped)
+
+        def quantize_dealt(raw, grouped):
+            deal(nc.scalar.copy, grouped, raw, 0, P)
             return quantize(grouped)
 
         def gather(window, offsets, dtype, name):
@@ -237,121 +223,140 @@ def tile_list_groove_fault_ledger_kernel(
             )
             return w2_q, (words, planes)
 
-        def heat_tile(i, w2_q, w3_q, product=None):
+        def heat_product(i, w2_q, w3_q, product=None):
             cols = slice(P * (i % PACK), P * (i % PACK + 1))
-            wg = wg2_first[:, 0, :] if i % PACK == 0 else wg2_rest[:, i % PACK - 1, :]
             first = 2 * i if i < PACK else 2 * (i % 2)
             bank_a, bank_b = banks[first], banks[first + 1]
             mx(bank_a[:], w2_q[0][:, cols], w2_q[1][:, cols], v2_w[:], v2_s[:], True, True)
             mx(bank_b[:], w3_q[0][:, cols], w3_q[1][:, cols], v2_w[:], v2_s[:], True, True)
-            h2 = rotating("h2", 4, [P, S], F32)
+            h2 = rotating("h2", 5, [P, S], F32)
             nc.scalar.activation(h2[:], bank_a[:], ACT.Abs)
             if product is None:
                 product = h2[:]
             nc.vector.tensor_tensor(product, bank_b[:], h2[:], MULT)
+            return product
+
+        def heat_put(i, product):
+            wg = wg2_first[:, 0, :] if i % PACK == 0 else wg2_rest[:, i % PACK - 1, :]
             nc.vector.tensor_tensor(pages[i][:].indirect(idx4[:]), product, wg, MULT)
+
+        def heat_tile(i, w2_q, w3_q, product=None):
+            heat_put(i, heat_product(i, w2_q, w3_q, product))
+
+        work = held([P, PACK * S], F32, "work")
+
+        def spread_gate(rows, planes, dealt):
+            source = banks[4]
+            for b in range(S // P):
+                nc.tensor.transpose(source[:, P * b : P * (b + 1)], rows[:, P * b : P * (b + 1)], ident[:])
+            by_plane = source[:].rearrange("p (b q t) -> p b t q", b=S // P, t=PACK)
+            for n, t in enumerate(planes):
+                room = work[:, S * t : S * (t + 1)]
+                nc.scalar.copy(
+                    room.rearrange("p (b u q) -> p b u q", b=S // P, u=QUADS),
+                    by_plane[:, :, t, :].unsqueeze(2).to_broadcast([P, S // P, QUADS, QUAD]),
+                )
+                bank = banks[5 + (n + 1) % 3]
+                for b in range(S // P):
+                    nc.tensor.transpose(bank[:, P * b : P * (b + 1)], room[:, P * b : P * (b + 1)], ident[:])
+                nc.scalar.copy(dealt[:, n, :], bank[:])
 
         v_w = {}
         heat_w = prepare_heat(0)
-        heat_tile(0, *heat_w)
-        heat_tile(1, *heat_w)
+        products = [heat_product(i, *heat_w) for i in range(PACK)]
+        wg2_rest = rotating("gate", 1, [P, PACK - 1, S], F32)
+        spread_gate(wg2_rows, (1, 2, 3), wg2_rest)
+        heat_put(0, products[0])
+        heat_put(1, products[1])
         heat_w_next = prepare_heat(1)
-        heat_tile(2, *heat_w)
+        wg1_dealt = held([P, PACK, S], F32, "wg1_dealt")
+        heat_put(2, products[2])
         v_w[0] = gather(tabs[0], idx, U32, "v_w0")
-        heat_tile(3, *heat_w)
+        heat_put(3, products[3])
         v_w[1] = gather(tabs[1], idx, U32, "v_w1")
         heat_tile(4, *heat_w_next)
+        spread_gate(wg1_rows, range(PACK), wg1_dealt)
         v_s = gather(tab_s, idx, U8, "v_s")
         w1_q = {}
-        w1_q[0, 0] = quantize_plain(w1_raw[0, 0], staged([P, PACK * S], BF16))
+        w1_q[0, 0] = quantize_dealt(w1_raw[0, 0], staged([P, PACK * S], BF16))
         v_w[2] = gather(tabs[2], idx, U32, "v_w2")
         heat_tile(5, *heat_w_next)
-        w1_q[0, 1] = quantize_plain(w1_raw[0, 1], staged([P, PACK * S], BF16))
+        w1_q[0, 1] = quantize_dealt(w1_raw[0, 1], staged([P, PACK * S], BF16))
+        heat_tile(6, *heat_w_next)
         grouped = staged([P, PACK * S], BF16)
-        w1_q[0, 2] = quantize_plain(w1_raw[0, 2], grouped)
-        late = grouped[:].bitcast(F32)
-        heat_tile(6, *heat_w_next, late[:, 0:S])
-        heat_tile(7, *heat_w_next, late[:, S : 2 * S])
+        w1_q[0, 2] = quantize_dealt(w1_raw[0, 2], grouped)
+        last_product = heat_product(7, *heat_w_next, grouped[:].bitcast(F32)[:, 0:S])
 
-        work = held([P, PACK * S], F32, "work")
-        y_t = work[:].rearrange("p (b t q) -> p b t q", b=S // P, t=PACK)
-        x_planes = work[:].rearrange("p (t j) -> p t j", t=PACK)
+        for kp in range(K_PASSES):
+            w1_raw[1, kp] = load_weight(w1, kp, S)
+        w5_raw[0] = load_weight(w5, 0, 0)
+        master_hi = big([P, PACK, S], F32)
+        nc.sync.dma_start(master_hi[:], master[PASS:H, :].rearrange("(p t) j -> p t j", t=PACK))
+        for i in range(PACK):
+            masters[PACK + i] = master_hi[:, i, :]
+        w5_raw[1] = load_weight(w5, 1, 0)
+        w5_raw[2] = load_weight(w5, 2, 0)
+        lots_t = rotating("gate", 1, [P, N // P, S], F32)
+        nc.sync.dma_start(lots_t[:], lots.rearrange("(b p) j -> p b j", p=P))
+        w4_w = small([P, R_PASSES, 2 * N], U8)
+        nc.sync.dma_start(w4_w[:].bitcast(I32), w4_words.rearrange("a p b -> p a b").bitcast(I32))
 
-        def turn_master(i, turned):
-            bank = banks[i % PACK]
-            for b in range(S // P):
-                nc.tensor.transpose(bank[:, P * b : P * (b + 1)], masters[i][:, P * b : P * (b + 1)], ident[:])
-            nc.scalar.copy(turned, bank[:])
+        for q in range(QUADS):
+            nc.sync.dma_start(
+                w4_s[QUAD * q : QUAD * q + 4, :, :].bitcast(I32),
+                w4_scales[:, 4 * q : 4 * q + 4, :].rearrange("a r n -> r a n").bitcast(I32),
+            )
 
-        def stamper_products(a):
+        x_planes = w1_raw[1, 2]
+
+        def stamper_passes(a):
             for kp in range(K_PASSES):
                 codes, scales = w1_q[a, kp]
-                for b in range(S // P):
-                    cols = slice(P * b, P * (b + 1))
-                    mx(banks[4 + b][:], v_w[kp][:, cols], v_s[4 * kp : P, cols], codes[:], scales[:], kp == 0, kp == K_PASSES - 1)
-            for b in range(S // P):
-                nc.scalar.copy(y_t[:, b, :, :], banks[4 + b][:].rearrange("p (q t) -> p t q", t=PACK))
+                for t in range(PACK):
+                    cols = slice(P * t, P * (t + 1))
+                    mx(banks[4 + t][:], codes[:, cols], scales[:, cols], v_w[kp][:], v_s[4 * kp : P, :], kp == 0, kp == K_PASSES - 1)
 
-        def stamper_sum(i, turned):
-            t = i % PACK
-            bank = banks[t]
-            for b in range(S // P):
-                cols = slice(P * b, P * (b + 1))
-                nc.tensor.matmul(bank[:, cols], turned[:, cols], ident[:], is_transpose=True, start=True, stop=False)
-                nc.tensor.matmul(bank[:, cols], y_t[:, b, t, :], ident[:], is_transpose=True, start=False, stop=True)
+        def stamper_sum(i):
+            nc.vector.tensor_tensor(masters[i][:, :], banks[4 + i % PACK][:], masters[i][:, :], ADD)
 
-        def stamper_tile(i, turned, h1=None):
-            stamper_sum(i, turned)
-            if h1 is None:
-                h1 = rotating("h1", 4, [P, S], F32)[:]
-            nc.scalar.activation(h1, banks[i % PACK][:], ACT.Silu)
-            return h1
+        def stamper_silu(i, h1):
+            nc.scalar.activation(h1, masters[i][:, :], ACT.Silu)
 
         def put(i, h1):
-            t = i % PACK
-            wg = wg1_lo if t < 2 else wg1_hi
-            nc.vector.tensor_tensor(pages[i][:].indirect(idx3[:]), h1, wg[:, t % 2, :], MULT)
+            nc.vector.tensor_tensor(pages[i][:].indirect(idx3[:]), h1, wg1_dealt[:, i % PACK, :], MULT)
 
-        def fetch(i, picked=None):
-            if picked is None:
-                picked = rotating("picked", 4, [P, S], F32)[:]
+        def fetch(i, picked):
             nc.vector.tensor_copy(picked, pages[i][:].indirect(idx5[:]))
             return picked
 
-        def listen(i, picked, c0, c1):
+        def listen(i, picked):
             a, t = i // PACK, i % PACK
-            nc.scalar.activation(x_planes[:, t, c0:c1], picked[:, c0:c1], ACT.Tanh)
-            nc.scalar.activation(x_planes[:, t, c0:c1], x_planes[:, t, c0:c1], ACT.Copy, scale=gain_t[:, a, t : t + 1])
+            nc.scalar.activation(x_planes[:, t, :], picked, ACT.Tanh)
+            nc.scalar.activation(x_planes[:, t, :], x_planes[:, t, :], ACT.Copy, scale=gain_t[:, a, t : t + 1])
 
-        h1s, picks = {}, {}
-        turned_lo = w1_raw[0, 2]
-        turned = [turned_lo[:, t, :] for t in range(PACK)]
-        turn_master(0, turned[0])
-        stamper_products(0)
-        for i in (1, 2, 3):
-            turn_master(i, turned[i])
+        def picked_tile():
+            return rotating("picked", 4, [P, S], F32)
+
+        stamper_passes(0)
+        for i in range(PACK):
+            stamper_sum(i)
         for i in (0, 1):
-            put(i, stamper_tile(i, turned[i]))
-        w1_q[1, 0] = quantize_plain(w1_raw[1, 0], bf16_room(w1_raw[0, 2]))
-        w1_q[1, 1] = quantize_plain(w1_raw[1, 1], bf16_room(w1_raw[1, 0]))
-        w1_q[1, 2] = quantize_plain(w1_raw[1, 2], bf16_room(w1_raw[1, 1]))
-        late = w1_raw[1, 2]
+            stamper_silu(i, masters[i][:, :])
+        heat_put(7, last_product)
         for i in (0, 1):
-            picks[i] = fetch(i, late[:, i, :])
+            put(i, masters[i][:, :])
+        picks = [fetch(i, picked_tile()[:]) for i in (0, 1)]
+        for kp in range(K_PASSES):
+            w1_q[1, kp] = quantize_dealt(w1_raw[1, kp], staged([P, PACK * S], BF16))
+        stamper_passes(1)
         for i in (2, 3):
-            put(i, stamper_tile(i, turned[i], late[:, i, :]))
-        for i in (2, 3):
-            picks[i] = fetch(i)
-        turned_hi = w1_raw[1, 1]
-        turned = [turned_hi[:, t, :] for t in range(PACK)]
-        turn_master(4, turned[0])
-        stamper_products(1)
-        for i in range(4, 7):
-            if i > 4:
-                turn_master(i, turned[i - 4])
-            h1s[i] = stamper_tile(i, turned[i - 4], late[:, i - 2, :] if i < 6 else None)
-        turn_master(7, turned[3])
-        stamper_sum(7, turned[3])
+            stamper_silu(i, x_planes[:, i, :])
+            put(i, x_planes[:, i, :])
+        for i in range(PACK, 2 * PACK):
+            stamper_sum(i)
+            if i < 7:
+                stamper_silu(i, masters[i][:, :])
+        picks.extend(fetch(i, x_planes[:, i, :]) for i in (2, 3))
 
         def sum_range(b, half):
             c0 = HALF * (b % 2)
@@ -365,7 +370,7 @@ def tile_list_groove_fault_ledger_kernel(
                     rows = slice(P * b, P * (b + 1))
                     mx(
                         bank[:, c0 : c0 + HALF], w5_q[0][:, rows], w5_q[1][:, rows],
-                        v_w[kp][:, cols], v_s[4 * kp : P, cols], kp == FIRST_PASS and b % 2 == 0, False,
+                        v_w[kp][:, cols], v_s[4 * kp : P, cols], kp == 0 and b % 2 == 0, False,
                     )
 
         def listener_passes(a, x_q, half):
@@ -381,25 +386,25 @@ def tile_list_groove_fault_ledger_kernel(
                     )
 
         w5_q = [
-            quantize_plain(w5_raw[0], bf16_room(master_hi, 1)),
-            quantize_plain(w5_raw[1], bf16_room(turned_hi, 1)),
-            quantize_plain(w5_raw[2], bf16_room(w5_raw[1])),
+            quantize_plain(w5_raw[0], bf16_room(w1_raw[1, 0])),
+            quantize_plain(w5_raw[1], bf16_room(w1_raw[1, 0], 1)),
+            quantize_plain(w5_raw[2], bf16_room(w1_raw[1, 1])),
         ]
-        for i in range(4):
-            listen(i, picks[i], 0, S)
-        grouped = staged([P, PACK * S], BF16)
-        interleave(nc.scalar.copy, grouped, x_planes, 0, S)
+        for i in range(PACK):
+            listen(i, picks[i])
+        grouped = bf16_room(w1_raw[1, 1], 1)
+        interleave(nc.scalar.copy, grouped, x_planes[:], 0, S)
         last = x_planes[:, PACK - 1, :]
-        nc.scalar.activation(last, banks[PACK - 1][:], ACT.Silu)
+        stamper_silu(7, last)
         for i in range(4, 7):
-            put(i, h1s[i])
+            put(i, masters[i][:, :])
         x_q = quantize(grouped)
-        for kp in (1, 2, 0):
+        for kp in range(K_PASSES):
             ledger_passes(kp, w5_q[kp])
         for half in range(2):
             listener_passes(0, x_q, half)
         for i in (4, 5):
-            listen(i, fetch(i), 0, S)
+            listen(i, fetch(i, picked_tile()[:]))
         picked = rotating("picked", 4, [P, S], F32)
         fetch(6, x_planes[:, 2, :])
         nc.scalar.activation(picked[:], x_planes[:, 2, :], ACT.Tanh)
@@ -416,9 +421,9 @@ def tile_list_groove_fault_ledger_kernel(
         for half in range(2):
             c0 = HALF * half
             split = c0 + (HALF if half == 0 else VECTOR_COLS)
-            interleave(nc.vector.tensor_copy, grouped, x_planes, c0, split, c0)
+            interleave(nc.vector.tensor_copy, grouped, x_planes[:], c0, split, c0)
             if split < c0 + HALF:
-                interleave(nc.scalar.copy, grouped, x_planes, split, c0 + HALF, c0)
+                interleave(nc.scalar.copy, grouped, x_planes[:], split, c0 + HALF, c0)
             nc.vector.quantize_mx(
                 out=x_q[0][:, c0 : c0 + HALF].bitcast(FP8X4), scales=x_q[1][:, c0 : c0 + HALF],
                 in_=grouped[:, 0 : PACK * HALF],

@@ -26,6 +26,7 @@ R_PASSES = H // PASS
 QUADS = 4
 QUAD = 32
 HALF = S // 2
+HEAT_BANKS = (0, 2, 2, 6, 6, 2, 6, 2)
 HEAD_VECTOR_ROWS = 56
 VECTOR_COLS = 160
 
@@ -156,8 +157,8 @@ def tile_list_groove_fault_ledger_kernel(
         nc.sync.dma_start(gain_t[:], gain.rearrange("(a p t) -> p a t", a=R_PASSES, t=PACK))
         w1_raw[0, 1] = load_weight(w1, 1, 0)
         pages[6] = load_page(6)
-        masters[0] = load_master(0)
         w1_raw[0, 2] = load_weight(w1, 2, 0)
+        masters[0] = load_master(0)
         pages[7] = load_page(7)
         masters[1] = load_master(1)
         masters[2] = load_master(2)
@@ -223,13 +224,13 @@ def tile_list_groove_fault_ledger_kernel(
             )
             return w2_q, (words, planes)
 
-        def heat_product(i, w2_q, w3_q, product=None):
+        def heat_product(i, w2_q, w3_q, product=None, swing=None):
             cols = slice(P * (i % PACK), P * (i % PACK + 1))
-            first = 2 * i if i < PACK else 2 * (i % 2)
+            first = HEAT_BANKS[i]
             bank_a, bank_b = banks[first], banks[first + 1]
             mx(bank_a[:], w2_q[0][:, cols], w2_q[1][:, cols], v2_w[:], v2_s[:], True, True)
             mx(bank_b[:], w3_q[0][:, cols], w3_q[1][:, cols], v2_w[:], v2_s[:], True, True)
-            h2 = rotating("h2", 5, [P, S], F32)
+            h2 = rotating("h2", 5, [P, S], F32) if swing is None else swing
             nc.scalar.activation(h2[:], bank_a[:], ACT.Abs)
             if product is None:
                 product = h2[:]
@@ -245,10 +246,15 @@ def tile_list_groove_fault_ledger_kernel(
 
         work = held([P, PACK * S], F32, "work")
 
-        def spread_gate(rows, planes, dealt):
-            source = banks[4]
+        def turn(bank, rows):
             for b in range(S // P):
-                nc.tensor.transpose(source[:, P * b : P * (b + 1)], rows[:, P * b : P * (b + 1)], ident[:])
+                nc.tensor.transpose(bank[:, P * b : P * (b + 1)], rows[:, P * b : P * (b + 1)], ident[:])
+
+        def turn_gate(rows):
+            turn(banks[4], rows)
+            return banks[4]
+
+        def spread_gate(source, planes, dealt, outs):
             by_plane = source[:].rearrange("p (b q t) -> p b t q", b=S // P, t=PACK)
             for n, t in enumerate(planes):
                 room = work[:, S * t : S * (t + 1)]
@@ -256,17 +262,19 @@ def tile_list_groove_fault_ledger_kernel(
                     room.rearrange("p (b u q) -> p b u q", b=S // P, u=QUADS),
                     by_plane[:, :, t, :].unsqueeze(2).to_broadcast([P, S // P, QUADS, QUAD]),
                 )
-                bank = banks[5 + (n + 1) % 3]
-                for b in range(S // P):
-                    nc.tensor.transpose(bank[:, P * b : P * (b + 1)], room[:, P * b : P * (b + 1)], ident[:])
+                bank = banks[outs[n]]
+                turn(bank, room)
                 nc.scalar.copy(dealt[:, n, :], bank[:])
 
         v_w = {}
         heat_w = prepare_heat(0)
-        products = [heat_product(i, *heat_w) for i in range(PACK)]
-        wg2_rest = rotating("gate", 1, [P, PACK - 1, S], F32)
-        spread_gate(wg2_rows, (1, 2, 3), wg2_rest)
+        products = [heat_product(0, *heat_w)]
         heat_put(0, products[0])
+        wg2_rest = rotating("gate", 1, [P, PACK - 1, S], F32)
+        source = turn_gate(wg2_rows)
+        products.append(heat_product(1, *heat_w, None, wg2_rows))
+        spread_gate(source, (1, 2, 3), wg2_rest, (5, 6, 7))
+        products.extend(heat_product(i, *heat_w) for i in (2, 3))
         heat_put(1, products[1])
         heat_w_next = prepare_heat(1)
         wg1_dealt = held([P, PACK, S], F32, "wg1_dealt")
@@ -275,7 +283,7 @@ def tile_list_groove_fault_ledger_kernel(
         heat_put(3, products[3])
         v_w[1] = gather(tabs[1], idx, U32, "v_w1")
         heat_tile(4, *heat_w_next)
-        spread_gate(wg1_rows, range(PACK), wg1_dealt)
+        spread_gate(turn_gate(wg1_rows), range(PACK), wg1_dealt, (5, 0, 1, 5))
         v_s = gather(tab_s, idx, U8, "v_s")
         w1_q = {}
         w1_q[0, 0] = quantize_dealt(w1_raw[0, 0], staged([P, PACK * S], BF16))
@@ -287,11 +295,11 @@ def tile_list_groove_fault_ledger_kernel(
         w1_q[0, 2] = quantize_dealt(w1_raw[0, 2], grouped)
         last_product = heat_product(7, *heat_w_next, grouped[:].bitcast(F32)[:, 0:S])
 
+        master_hi = big([P, PACK, S], F32)
+        nc.sync.dma_start(master_hi[:], master[PASS:H, :].rearrange("(p t) j -> p t j", t=PACK))
         for kp in range(K_PASSES):
             w1_raw[1, kp] = load_weight(w1, kp, S)
         w5_raw[0] = load_weight(w5, 0, 0)
-        master_hi = big([P, PACK, S], F32)
-        nc.sync.dma_start(master_hi[:], master[PASS:H, :].rearrange("(p t) j -> p t j", t=PACK))
         for i in range(PACK):
             masters[PACK + i] = master_hi[:, i, :]
         w5_raw[1] = load_weight(w5, 1, 0)
@@ -309,9 +317,9 @@ def tile_list_groove_fault_ledger_kernel(
 
         x_planes = w1_raw[1, 2]
 
-        def stamper_passes(a):
+        def stamper_passes():
             for kp in range(K_PASSES):
-                codes, scales = w1_q[a, kp]
+                codes, scales = w1_q[0, kp]
                 for t in range(PACK):
                     cols = slice(P * t, P * (t + 1))
                     mx(banks[4 + t][:], codes[:, cols], scales[:, cols], v_w[kp][:], v_s[4 * kp : P, :], kp == 0, kp == K_PASSES - 1)
@@ -320,7 +328,32 @@ def tile_list_groove_fault_ledger_kernel(
             nc.vector.tensor_tensor(masters[i][:, :], banks[4 + i % PACK][:], masters[i][:, :], ADD)
 
         def stamper_silu(i, h1):
-            nc.scalar.activation(h1, masters[i][:, :], ACT.Silu)
+            nc.scalar.activation(h1, masters[i][:, :] if i < PACK else banks[i - PACK][:], ACT.Silu)
+
+        y_turned = work[:].rearrange("p (b t q) -> p b t q", b=S // P, t=PACK)
+        master_turned = w1_raw[0, 2]
+
+        def turn_master(t):
+            turn(banks[t], masters[PACK + t])
+            nc.scalar.copy(master_turned[:, t, :], banks[t][:])
+
+        def turned_passes():
+            for kp in range(K_PASSES):
+                codes, scales = w1_q[1, kp]
+                for b in range(S // P):
+                    cols = slice(P * b, P * (b + 1))
+                    mx(banks[4 + b][:], v_w[kp][:, cols], v_s[4 * kp : P, cols], codes[:], scales[:], kp == 0, kp == K_PASSES - 1)
+            for b in range(S // P):
+                nc.scalar.copy(y_turned[:, b, :, :], banks[4 + b][:].rearrange("p (q t) -> p t q", t=PACK))
+
+        def turned_sum(t):
+            for b in range(S // P):
+                cols = slice(P * b, P * (b + 1))
+                nc.tensor.matmul(banks[t][:, cols], master_turned[:, t, cols], ident[:], is_transpose=True, start=b == 0, stop=False)
+            order = list(range(S // P)) if t == 0 else list(reversed(range(S // P)))
+            for b in order:
+                cols = slice(P * b, P * (b + 1))
+                nc.tensor.matmul(banks[t][:, cols], y_turned[:, b, t, :], ident[:], is_transpose=True, start=False, stop=b == order[-1])
 
         def put(i, h1):
             nc.vector.tensor_tensor(pages[i][:].indirect(idx3[:]), h1, wg1_dealt[:, i % PACK, :], MULT)
@@ -337,7 +370,7 @@ def tile_list_groove_fault_ledger_kernel(
         def picked_tile():
             return rotating("picked", 4, [P, S], F32)
 
-        stamper_passes(0)
+        stamper_passes()
         for i in range(PACK):
             stamper_sum(i)
         for i in (0, 1):
@@ -345,17 +378,20 @@ def tile_list_groove_fault_ledger_kernel(
         heat_put(7, last_product)
         for i in (0, 1):
             put(i, masters[i][:, :])
-        picks = [fetch(i, picked_tile()[:]) for i in (0, 1)]
-        for kp in range(K_PASSES):
-            w1_q[1, kp] = quantize_dealt(w1_raw[1, kp], staged([P, PACK * S], BF16))
-        stamper_passes(1)
+        for kp in (0, 1):
+            w1_q[1, kp] = quantize_plain(w1_raw[1, kp], staged([P, PACK * S], BF16))
+        picks = [fetch(i, w1_raw[1, 1][:, i, :]) for i in (0, 1)]
+        w1_q[1, 2] = quantize_plain(w1_raw[1, 2], staged([P, PACK * S], BF16))
         for i in (2, 3):
             stamper_silu(i, x_planes[:, i, :])
             put(i, x_planes[:, i, :])
-        for i in range(PACK, 2 * PACK):
-            stamper_sum(i)
-            if i < 7:
-                stamper_silu(i, masters[i][:, :])
+        for t in range(PACK):
+            turn_master(t)
+        turned_passes()
+        for t in range(PACK):
+            turned_sum(t)
+            if t < PACK - 1:
+                stamper_silu(PACK + t, masters[PACK + t])
         picks.extend(fetch(i, x_planes[:, i, :]) for i in (2, 3))
 
         def sum_range(b, half):
@@ -370,7 +406,7 @@ def tile_list_groove_fault_ledger_kernel(
                     rows = slice(P * b, P * (b + 1))
                     mx(
                         bank[:, c0 : c0 + HALF], w5_q[0][:, rows], w5_q[1][:, rows],
-                        v_w[kp][:, cols], v_s[4 * kp : P, cols], kp == 0 and b % 2 == 0, False,
+                        v_w[kp][:, cols], v_s[4 * kp : P, cols], kp == 1 and b % 2 == 0, False,
                     )
 
         def listener_passes(a, x_q, half):
@@ -386,9 +422,9 @@ def tile_list_groove_fault_ledger_kernel(
                     )
 
         w5_q = [
-            quantize_plain(w5_raw[0], bf16_room(w1_raw[1, 0])),
-            quantize_plain(w5_raw[1], bf16_room(w1_raw[1, 0], 1)),
-            quantize_plain(w5_raw[2], bf16_room(w1_raw[1, 1])),
+            quantize_plain(w5_raw[0], bf16_room(master_turned)),
+            quantize_plain(w5_raw[1], bf16_room(master_turned, 1)),
+            quantize_plain(w5_raw[2], bf16_room(w5_raw[1])),
         ]
         for i in range(PACK):
             listen(i, picks[i])
@@ -399,7 +435,7 @@ def tile_list_groove_fault_ledger_kernel(
         for i in range(4, 7):
             put(i, masters[i][:, :])
         x_q = quantize(grouped)
-        for kp in range(K_PASSES):
+        for kp in (1, 0, 2):
             ledger_passes(kp, w5_q[kp])
         for half in range(2):
             listener_passes(0, x_q, half)

from contextlib import ExitStack

import concourse.mybir as mybir
from concourse.masks import make_identity

K, M, H, N, T, T3, S, T2 = 1536, 512, 1024, 512, 2048, 1024, 512, 2048
FLOPS = 2 * S * (K * H + 2 * M * H + H * N + K * N)

F32 = mybir.dt.float32
BF16 = mybir.dt.bfloat16
I32 = mybir.dt.int32
U32 = mybir.dt.uint32
U16 = mybir.dt.uint16
U8 = mybir.dt.uint8
FP8X4 = mybir.dt.float8_e4m3fn_x4
FP4X4 = mybir.dt.float4_e2m1fn_x4
ACT = mybir.ActivationFunctionType
MULT = mybir.AluOpType.mult
ADD = mybir.AluOpType.add

P = 128
PACK = 4
PASS = P * PACK
K_PASSES = K // PASS
R_PASSES = H // PASS
QUADS = 4
QUAD = 32
HALF = S // 2
HEAT_BANKS = (0, 2, 2, 6, 6, 2, 6, 2)
HEAD_VECTOR_ROWS = 56
VECTOR_COLS = 160


def tile_list_groove_fault_ledger_kernel(
    tc, tab_words, tab_scales, tab2_words, tab2_scales, offs, offs2, offs3, offs4, offs5,
    w1, master, w2, w3_words, w3_scales, wg1, wg2, page0, gain, w4_words, w4_scales, w5, lots, out,
):
    nc = tc.nc
    with ExitStack() as ctx:
        lists = ctx.enter_context(tc.tile_pool(name="lists", bufs=1))
        keep = ctx.enter_context(tc.tile_pool(name="keep", bufs=1))
        ring = ctx.enter_context(tc.tile_pool(name="ring", bufs=1))
        psum = ctx.enter_context(tc.psum_pool(name="psum", bufs=1))

        banks = [psum.tile([P, S], F32, name="bank%d" % b) for b in range(8)]

        def held(shape, dtype, name):
            return keep.tile(shape, dtype, name=name, align_bytes=64)

        turns = {}

        def rotating(kind, depth, shape, dtype, slot=None):
            if slot is None:
                slot = turns.get(kind, 0) % depth
                turns[kind] = slot + 1
            name = "%s%d" % (kind, slot)
            return ring.tile(shape, dtype, name=name, tag=name, align_bytes=64)

        def big(shape, dtype):
            return rotating("big", 8, shape, dtype)

        def small(shape, dtype):
            return rotating("small", 4, shape, dtype)

        def staged(shape, dtype):
            return rotating("staged", 3, shape, dtype)

        def words_tile(dtype):
            return rotating("codes", 8, [P, S], dtype)

        tab2_s = held([P, T3], U8, "tab2_s")
        w3_s = held([P, H], U8, "w3_s")
        tab_s = held([P, T], U8, "tab_s")
        nc.gpsimd.memset(tab2_s[:].bitcast(I32), 0)
        nc.gpsimd.memset(w3_s[:].bitcast(I32), 0)

        def load_list(src, name):
            t = lists.tile([P, S // 16], U16, name=name)
            nc.sync.dma_start(t[:], src)
            return t

        def load_scale_rows(queue, dst, src):
            for q in range(QUADS):
                queue.dma_start(dst[QUAD * q : QUAD * q + 4, :].bitcast(I32), src[4 * q : 4 * q + 4, :].bitcast(I32))

        def load_weight(w, kp, c0):
            raw = big([P, PACK, S], F32)
            nc.sync.dma_start(raw[:], w[PASS * kp : PASS * (kp + 1), c0 : c0 + S].rearrange("(p j) c -> p j c", j=PACK))
            return raw

        page_rows = page0.rearrange("(a p t) s -> a t p s", a=R_PASSES, t=PACK)
        master_rows = master.rearrange("(a p t) s -> a t p s", a=R_PASSES, t=PACK)

        def load_page(i):
            t = keep.tile([P, T2], F32, name="page%d" % i)
            nc.sync.dma_start(t[:], page_rows[i // PACK][i % PACK])
            return t

        def load_master(i):
            t = small([P, S], F32)
            nc.sync.dma_start(t[:], master_rows[i // PACK][i % PACK])
            return t

        def load_wg(src, t0, t1, t):
            rows = src.rearrange("(q t) j -> q t j", t=PACK)
            for q in (0, 2, 1, 3):
                nc.sync.dma_start(t[QUAD * q : QUAD * (q + 1), :, :], rows[:, t0:t1, :])
            return t

        def load_tab(kp):
            t = big([P, T], U32)
            nc.sync.dma_start(t[:].bitcast(I32), tab_words[kp].rearrange("p n t -> p (n t)").bitcast(I32))
            return t

        pages, masters, tabs = {}, {}, {}
        w1_raw, w2_raw, w5_raw = {}, {}, {}

        nc.gpsimd.memset(tab_s[:].bitcast(I32), 0)
        w4_s = held([P, R_PASSES, N], U8, "w4_s")
        nc.gpsimd.memset(w4_s[:].bitcast(I32), 0)
        ident = held([P, P], F32, "ident")
        make_identity(nc, ident[:])

        idx2 = load_list(offs2, "idx2")
        tab2_w = staged([P, T3], U32)
        nc.sync.dma_start(tab2_w[:].bitcast(I32), tab2_words[0].rearrange("p n t -> p (n t)").bitcast(I32))
        load_scale_rows(nc.sync, tab2_s, tab2_scales[0])
        w2_raw[0] = load_weight(w2, 0, 0)
        w3_raw = rotating("staged", 3, [P, H], I32, 2)
        nc.sync.dma_start(w3_raw[:], w3_words[0].rearrange("p n t -> p (n t)").bitcast(I32))
        load_scale_rows(nc.sync, w3_s, w3_scales[0])
        pages[0] = load_page(0)
        wg2_first = load_wg(wg2, 0, 1, held([P, 1, S], F32, "wg2_first"))
        idx4 = load_list(offs4, "idx4")
        wg2_rows = small([P, S], F32)
        nc.sync.dma_start(wg2_rows[:], wg2)
        pages[1] = load_page(1)
        pages[2] = load_page(2)
        w2_raw[1] = load_weight(w2, 0, S)
        idx = load_list(offs, "idx")
        tabs[0] = load_tab(0)
        pages[3] = load_page(3)
        wg1_rows = small([P, S], F32)
        nc.sync.dma_start(wg1_rows[:], wg1)
        idx3 = load_list(offs3, "idx3")
        tabs[1] = load_tab(1)
        idx5 = load_list(offs5, "idx5")
        pages[4] = load_page(4)
        for q in range(QUADS):
            nc.sync.dma_start(
                tab_s[QUAD * q : QUAD * q + 4 * K_PASSES, :].bitcast(I32), tab_scales[:, 4 * q : 4 * q + 4, :].bitcast(I32)
            )
        tabs[2] = load_tab(2)
        w1_raw[0, 0] = load_weight(w1, 0, 0)
        pages[5] = load_page(5)
        gain_t = held([P, R_PASSES, PACK], F32, "gain_t")
        nc.sync.dma_start(gain_t[:], gain.rearrange("(a p t) -> p a t", a=R_PASSES, t=PACK))
        w1_raw[0, 1] = load_weight(w1, 1, 0)
        pages[6] = load_page(6)
        w1_raw[0, 2] = load_weight(w1, 2, 0)
        masters[0] = load_master(0)
        pages[7] = load_page(7)
        masters[1] = load_master(1)
        masters[2] = load_master(2)
        masters[3] = load_master(3)

        def quantize(grouped):
            codes = words_tile(U32)
            scales = rotating("scales", 6, [P, S], U8)
            nc.vector.quantize_mx(out=codes[:].bitcast(FP8X4), scales=scales[:], in_=grouped[:])
            return codes, scales

        def interleave(copy, grouped, planes, c0, c1, base=0):
            dst = grouped[:, PACK * (c0 - base) : PACK * (c1 - base)].rearrange("p (c i j) -> p c j i", i=4, j=PACK)
            copy(dst, planes[:, :, c0:c1].rearrange("p j (c i) -> p c j i", i=4))

        def deal(copy, grouped, raw, m0, m1):
            dst = grouped[:].rearrange("p (t m j) -> p m t j", t=PACK, j=PACK)
            copy(dst[:, m0:m1, :, :], raw[:].rearrange("p j (m t) -> p m t j", t=PACK)[:, m0:m1, :, :])

        def bf16_room(spent, upper=0):
            return spent[:].rearrange("p j c -> p (j c)").bitcast(BF16)[:, PACK * S * upper : PACK * S * (upper + 1)]

        def quantize_plain(raw, grouped):
            interleave(nc.scalar.copy, grouped, raw[:], 0, S)
            return quantize(grouped)

        def quantize_dealt(raw, grouped):
            deal(nc.scalar.copy, grouped, raw, 0, P)
            return quantize(grouped)

        def gather(window, offsets, dtype, name):
            t = held([P, S], dtype, name)
            nc.vector.tensor_copy(t[:], window[:].indirect(offsets[:]))
            return t

        def mx(bank, lhs, lhs_s, rhs, rhs_s, start, stop, lhs_dtype=FP8X4):
            nc.tensor.matmul_mx(
                out=bank, lhsT=lhs.bitcast(lhs_dtype), lhsT_scale=lhs_s, rhs=rhs.bitcast(FP8X4), rhs_scale=rhs_s,
                start=start, stop=stop,
            )

        v2_w = gather(tab2_w, idx2, U32, "v2_w")
        v2_s = gather(tab2_s, idx2, U8, "v2_s")

        w3_dealt = held([P, R_PASSES, S], I32, "w3_dealt")

        def prepare_heat(a):
            grouped = staged([P, PACK * S], BF16)
            if a == 0:
                deal(nc.vector.tensor_copy, grouped, w2_raw[a], 0, HEAD_VECTOR_ROWS)
                deal(nc.scalar.copy, grouped, w2_raw[a], HEAD_VECTOR_ROWS, P)
            else:
                deal(nc.scalar.copy, grouped, w2_raw[a], 0, P)
            w2_q = quantize(grouped)
            words = w3_dealt[:, a, :]
            nc.vector.tensor_copy(
                words.rearrange("p (t m) -> p t m", t=PACK), w3_raw[:, S * a : S * (a + 1)].rearrange("p (m t) -> p t m", t=PACK)
            )
            planes = held([P, S], U8, "w3_s_dealt%d" % a)
            nc.vector.tensor_copy(
                planes[:].rearrange("p (t m) -> p t m", t=PACK),
                w3_s[:, S * a : S * (a + 1)].rearrange("p (m t) -> p t m", t=PACK),
            )
            return w2_q, (words, planes)

        def heat_product(i, w2_q, w3_q, product=None, swing=None):
            cols = slice(P * (i % PACK), P * (i % PACK + 1))
            first = HEAT_BANKS[i]
            bank_a, bank_b = banks[first], banks[first + 1]
            mx(bank_a[:], w2_q[0][:, cols], w2_q[1][:, cols], v2_w[:], v2_s[:], True, True)
            mx(bank_b[:], w3_q[0][:, cols], w3_q[1][:, cols], v2_w[:], v2_s[:], True, True)
            h2 = rotating("h2", 5, [P, S], F32) if swing is None else swing
            nc.scalar.activation(h2[:], bank_a[:], ACT.Abs)
            if product is None:
                product = h2[:]
            nc.vector.tensor_tensor(product, bank_b[:], h2[:], MULT)
            return product

        def heat_put(i, product):
            wg = wg2_first[:, 0, :] if i % PACK == 0 else wg2_rest[:, i % PACK - 1, :]
            nc.vector.tensor_tensor(pages[i][:].indirect(idx4[:]), product, wg, MULT)

        def heat_tile(i, w2_q, w3_q, product=None):
            heat_put(i, heat_product(i, w2_q, w3_q, product))

        work = held([P, PACK * S], F32, "work")

        def turn(bank, rows):
            for b in range(S // P):
                nc.tensor.transpose(bank[:, P * b : P * (b + 1)], rows[:, P * b : P * (b + 1)], ident[:])

        def turn_gate(rows):
            turn(banks[4], rows)
            return banks[4]

        def spread_gate(source, planes, dealt, outs):
            by_plane = source[:].rearrange("p (b q t) -> p b t q", b=S // P, t=PACK)
            for n, t in enumerate(planes):
                room = work[:, S * t : S * (t + 1)]
                nc.scalar.copy(
                    room.rearrange("p (b u q) -> p b u q", b=S // P, u=QUADS),
                    by_plane[:, :, t, :].unsqueeze(2).to_broadcast([P, S // P, QUADS, QUAD]),
                )
                bank = banks[outs[n]]
                turn(bank, room)
                nc.scalar.copy(dealt[:, n, :], bank[:])

        v_w = {}
        heat_w = prepare_heat(0)
        products = [heat_product(0, *heat_w)]
        heat_put(0, products[0])
        wg2_rest = rotating("gate", 1, [P, PACK - 1, S], F32)
        source = turn_gate(wg2_rows)
        products.append(heat_product(1, *heat_w, None, wg2_rows))
        spread_gate(source, (1, 2, 3), wg2_rest, (5, 6, 7))
        products.extend(heat_product(i, *heat_w) for i in (2, 3))
        heat_put(1, products[1])
        heat_w_next = prepare_heat(1)
        wg1_dealt = held([P, PACK, S], F32, "wg1_dealt")
        heat_put(2, products[2])
        v_w[0] = gather(tabs[0], idx, U32, "v_w0")
        heat_put(3, products[3])
        v_w[1] = gather(tabs[1], idx, U32, "v_w1")
        heat_tile(4, *heat_w_next)
        spread_gate(turn_gate(wg1_rows), range(PACK), wg1_dealt, (5, 0, 1, 5))
        v_s = gather(tab_s, idx, U8, "v_s")
        w1_q = {}
        w1_q[0, 0] = quantize_dealt(w1_raw[0, 0], staged([P, PACK * S], BF16))
        v_w[2] = gather(tabs[2], idx, U32, "v_w2")
        heat_tile(5, *heat_w_next)
        w1_q[0, 1] = quantize_dealt(w1_raw[0, 1], staged([P, PACK * S], BF16))
        heat_tile(6, *heat_w_next)
        grouped = staged([P, PACK * S], BF16)
        w1_q[0, 2] = quantize_dealt(w1_raw[0, 2], grouped)
        last_product = heat_product(7, *heat_w_next, grouped[:].bitcast(F32)[:, 0:S])

        master_hi = big([P, PACK, S], F32)
        nc.sync.dma_start(master_hi[:], master[PASS:H, :].rearrange("(p t) j -> p t j", t=PACK))
        for kp in range(K_PASSES):
            w1_raw[1, kp] = load_weight(w1, kp, S)
        w5_raw[0] = load_weight(w5, 0, 0)
        for i in range(PACK):
            masters[PACK + i] = master_hi[:, i, :]
        w5_raw[1] = load_weight(w5, 1, 0)
        w5_raw[2] = load_weight(w5, 2, 0)
        lots_t = rotating("gate", 1, [P, N // P, S], F32)
        nc.sync.dma_start(lots_t[:], lots.rearrange("(b p) j -> p b j", p=P))
        w4_w = small([P, R_PASSES, 2 * N], U8)
        nc.sync.dma_start(w4_w[:].bitcast(I32), w4_words.rearrange("a p b -> p a b").bitcast(I32))

        for q in range(QUADS):
            nc.sync.dma_start(
                w4_s[QUAD * q : QUAD * q + 4, :, :].bitcast(I32),
                w4_scales[:, 4 * q : 4 * q + 4, :].rearrange("a r n -> r a n").bitcast(I32),
            )

        x_planes = w1_raw[1, 2]

        def stamper_passes():
            for kp in range(K_PASSES):
                codes, scales = w1_q[0, kp]
                for t in range(PACK):
                    cols = slice(P * t, P * (t + 1))
                    mx(banks[4 + t][:], codes[:, cols], scales[:, cols], v_w[kp][:], v_s[4 * kp : P, :], kp == 0, kp == K_PASSES - 1)

        def stamper_sum(i):
            nc.vector.tensor_tensor(masters[i][:, :], banks[4 + i % PACK][:], masters[i][:, :], ADD)

        def stamper_silu(i, h1):
            nc.scalar.activation(h1, masters[i][:, :] if i < PACK else banks[i - PACK][:], ACT.Silu)

        y_turned = work[:].rearrange("p (b t q) -> p b t q", b=S // P, t=PACK)
        master_turned = w1_raw[0, 2]

        def turn_master(t):
            turn(banks[t], masters[PACK + t])
            nc.scalar.copy(master_turned[:, t, :], banks[t][:])

        def turned_passes():
            for kp in range(K_PASSES):
                codes, scales = w1_q[1, kp]
                for b in range(S // P):
                    cols = slice(P * b, P * (b + 1))
                    mx(banks[4 + b][:], v_w[kp][:, cols], v_s[4 * kp : P, cols], codes[:], scales[:], kp == 0, kp == K_PASSES - 1)
            for b in range(S // P):
                nc.scalar.copy(y_turned[:, b, :, :], banks[4 + b][:].rearrange("p (q t) -> p t q", t=PACK))

        def turned_sum(t):
            for b in range(S // P):
                cols = slice(P * b, P * (b + 1))
                nc.tensor.matmul(banks[t][:, cols], master_turned[:, t, cols], ident[:], is_transpose=True, start=b == 0, stop=False)
            order = list(range(S // P)) if t == 0 else list(reversed(range(S // P)))
            for b in order:
                cols = slice(P * b, P * (b + 1))
                nc.tensor.matmul(banks[t][:, cols], y_turned[:, b, t, :], ident[:], is_transpose=True, start=False, stop=b == order[-1])

        def put(i, h1):
            nc.vector.tensor_tensor(pages[i][:].indirect(idx3[:]), h1, wg1_dealt[:, i % PACK, :], MULT)

        def fetch(i, picked):
            nc.vector.tensor_copy(picked, pages[i][:].indirect(idx5[:]))
            return picked

        def listen(i, picked):
            a, t = i // PACK, i % PACK
            nc.scalar.activation(x_planes[:, t, :], picked, ACT.Tanh)
            nc.scalar.activation(x_planes[:, t, :], x_planes[:, t, :], ACT.Copy, scale=gain_t[:, a, t : t + 1])

        def picked_tile():
            return rotating("picked", 4, [P, S], F32)

        stamper_passes()
        for i in range(PACK):
            stamper_sum(i)
        for i in (0, 1):
            stamper_silu(i, masters[i][:, :])
        heat_put(7, last_product)
        for i in (0, 1):
            put(i, masters[i][:, :])
        for kp in (0, 1):
            w1_q[1, kp] = quantize_plain(w1_raw[1, kp], staged([P, PACK * S], BF16))
        picks = [fetch(i, w1_raw[1, 1][:, i, :]) for i in (0, 1)]
        w1_q[1, 2] = quantize_plain(w1_raw[1, 2], staged([P, PACK * S], BF16))
        for i in (2, 3):
            stamper_silu(i, x_planes[:, i, :])
            put(i, x_planes[:, i, :])
        for t in range(PACK):
            turn_master(t)
        turned_passes()
        for t in range(PACK):
            turned_sum(t)
            if t < PACK - 1:
                stamper_silu(PACK + t, masters[PACK + t])
        picks.extend(fetch(i, x_planes[:, i, :]) for i in (2, 3))

        def sum_range(b, half):
            c0 = HALF * (b % 2)
            return banks[2 * half + b // 2], c0

        def ledger_passes(kp, w5_q):
            for half in range(2):
                cols = slice(HALF * half, HALF * (half + 1))
                for b in range(N // P):
                    bank, c0 = sum_range(b, half)
                    rows = slice(P * b, P * (b + 1))
                    mx(
                        bank[:, c0 : c0 + HALF], w5_q[0][:, rows], w5_q[1][:, rows],
                        v_w[kp][:, cols], v_s[4 * kp : P, cols], kp == 1 and b % 2 == 0, False,
                    )

        def listener_passes(a, x_q, half):
            for b in range(N // P):
                bank, c0 = sum_range(b, half)
                for piece in range(HALF // P):
                    cols = slice(HALF * half + P * piece, HALF * half + P * (piece + 1))
                    mx(
                        bank[:, c0 + P * piece : c0 + P * (piece + 1)],
                        w4_w[:, a, 2 * P * b : 2 * P * (b + 1)], w4_s[:, a, P * b : P * (b + 1)],
                        x_q[0][:, cols], x_q[1][:, cols],
                        False, a == R_PASSES - 1 and b % 2 == 1 and piece == HALF // P - 1, FP4X4,
                    )

        w5_q = [
            quantize_plain(w5_raw[0], bf16_room(master_turned)),
            quantize_plain(w5_raw[1], bf16_room(master_turned, 1)),
            quantize_plain(w5_raw[2], bf16_room(w5_raw[1])),
        ]
        for i in range(PACK):
            listen(i, picks[i])
        grouped = bf16_room(w1_raw[1, 1], 1)
        interleave(nc.scalar.copy, grouped, x_planes[:], 0, S)
        last = x_planes[:, PACK - 1, :]
        stamper_silu(7, last)
        for i in range(4, 7):
            put(i, masters[i][:, :])
        x_q = quantize(grouped)
        for kp in (1, 0, 2):
            ledger_passes(kp, w5_q[kp])
        for half in range(2):
            listener_passes(0, x_q, half)
        for i in (4, 5):
            listen(i, fetch(i, picked_tile()[:]))
        picked = rotating("picked", 4, [P, S], F32)
        fetch(6, x_planes[:, 2, :])
        nc.scalar.activation(picked[:], x_planes[:, 2, :], ACT.Tanh)
        nc.scalar.activation(x_planes[:, 2, :], picked[:], ACT.Copy, scale=gain_t[:, 1, 2:3])
        put(7, last)
        squashed = rotating("picked", 4, [P, HALF], F32)
        for half in range(2):
            c0 = HALF * half
            nc.vector.tensor_copy(picked[:, c0 : c0 + HALF], pages[7][:].indirect(idx5[:, c0 // 16 : (c0 + HALF) // 16]))
            nc.scalar.activation(squashed[:], picked[:, c0 : c0 + HALF], ACT.Tanh)
            nc.scalar.activation(x_planes[:, 3, c0 : c0 + HALF], squashed[:], ACT.Copy, scale=gain_t[:, 1, 3:4])
        grouped = staged([P, PACK * S], BF16)
        x_q = words_tile(U32), rotating("scales", 6, [P, S], U8)
        for half in range(2):
            c0 = HALF * half
            split = c0 + (HALF if half == 0 else VECTOR_COLS)
            interleave(nc.vector.tensor_copy, grouped, x_planes[:], c0, split, c0)
            if split < c0 + HALF:
                interleave(nc.scalar.copy, grouped, x_planes[:], split, c0 + HALF, c0)
            nc.vector.quantize_mx(
                out=x_q[0][:, c0 : c0 + HALF].bitcast(FP8X4), scales=x_q[1][:, c0 : c0 + HALF],
                in_=grouped[:, 0 : PACK * HALF],
            )
            listener_passes(1, x_q, half)
        out_rows = out.rearrange("(b p) j -> p b j", p=P)
        for half in range(2):
            cols = slice(HALF * half, HALF * (half + 1))
            for pair in range(2):
                rows = slice(2 * pair, 2 * pair + 2)
                sums = banks[2 * half + pair][:].rearrange("p (b j) -> p b j", b=2)
                nc.vector.tensor_tensor(lots_t[:, rows, cols], sums, lots_t[:, rows, cols], ADD)
                nc.sync.dma_start(out_rows[:, rows, cols], lots_t[:, rows, cols])
